import numpy as np
import ml_dtypes


def mxq(x, axis, fmt="e4m3"):
    dtype, down = {"e4m3": (ml_dtypes.float8_e4m3fn, 7), "e5m2": (ml_dtypes.float8_e5m2, 14)}[fmt]
    v = np.moveaxis(np.asarray(x, np.float32).astype(ml_dtypes.bfloat16).astype(np.float64), axis, -1)
    blocks = v.reshape(v.shape[:-1] + (-1, 32))
    amax = np.abs(blocks).max(-1, keepdims=True)
    byte = np.maximum(np.where(amax > 0, np.frexp(amax)[1] - 1 + 127, 0) - down, 1)
    scale = np.exp2(byte - 127.0)
    codes = (blocks / scale).astype(np.float32).astype(dtype).astype(np.float64)
    return np.moveaxis((codes * scale).reshape(v.shape), -1, axis)


WIDE = False


def mx_kscale(k, group=512):
    if not WIDE:
        return np.ones(k)
    levels = np.array([10, -10, 5, -5, 0])
    if group != 512:
        return np.exp2(np.random.permutation(np.resize(levels, k // group))).repeat(group)
    if k % 512:
        return np.exp2(np.random.permutation(np.resize(levels, k // 32))).repeat(32)
    a = np.empty((k // 512, 16))
    for p in range(k // 512):
        a[p, :8] = np.random.permutation(np.resize(levels, 8))
        for g in range(8):
            far = levels[np.abs(levels - a[p, g]) >= 10]
            a[p, g + 8] = far[np.random.randint(len(far))]
    return np.exp2(a.ravel()).repeat(32)


def f64(x):
    return np.asarray(x).astype(np.float64)


def striped(idx):
    return np.tile(np.asarray(idx).reshape(-1, 16).T, (8, 1)).astype(np.uint16)


def unstriped(offs):
    return offs[:16].T.reshape(-1).astype(np.int64)


H, KV, D, NQ, N = 2, 2, 256, 512, 512


def setup_inputs():
    n = np.random.standard_normal
    s = mx_kscale(D, 0)[:, None]
    u = mx_kscale(N)
    t = np.random.uniform(0.5, 2.0, N) * u
    v = n((KV, N, 128))
    return {
        "qT": (n((H, D, NQ)) * s * (0.70 / np.sqrt(D))).astype(np.float32),
        "kT": (n((KV, D, N)) / s).astype(np.float32),
        "t": t.reshape(N, 1).astype(np.float32),
        "v": (v / t[:, None]).astype(np.float32),
        "mask": (np.arange(N)[:, None] <= np.sort(np.random.randint(N // 4, N, NQ))[None, :]).astype(np.float32),
        "gn": np.tile(np.random.uniform(0.5, 2.0, 128), (128, 1)).astype(np.float32),
        "og": n((H, NQ, 128)).astype(np.float32),
    }


def reference(qT, kT, t, v, mask, gn, og):
    a = mxq(f64(kT), 1, "e4m3").transpose(0, 2, 1) @ mxq(f64(qT), 1, "e4m3")
    p = 1.0 / (1.0 + np.exp(-a))
    p = p * f64(mask)
    w = p * f64(t)
    y = mxq(w, 1, "e4m3").transpose(0, 2, 1) @ mxq(f64(v), 1, "e4m3")
    y = y / 16.0
    y = y / np.sqrt(np.mean(np.square(y), -1, keepdims=True) + 1e-5) * f64(gn)[:1]
    y = y / (1.0 + np.exp(-f64(og)))
    return y

@@ -1,0 +1,247 @@
+from contextlib import ExitStack
+
+import concourse.mybir as mybir
+
+H, D, NQ, N, E = 2, 256, 512, 512, 128
+FLOPS = 2 * H * N * NQ * D + 2 * H * NQ * N * E
+
+F32 = mybir.dt.float32
+BF16 = mybir.dt.bfloat16
+U32 = mybir.dt.uint32
+U8 = mybir.dt.uint8
+FP8X4 = mybir.dt.float8_e4m3fn_x4
+ACT = mybir.ActivationFunctionType
+ALU = mybir.AluOpType
+
+P = 128
+PACK = 4
+ROWS = D // PACK
+QB = 128
+BLOCKS = NQ // QB
+HALF = NQ // 2
+K_SPLIT = 88
+
+
+def tile_rows_a_sigmoid_mask_onorm_gate_kernel(tc, qT, kT, t, v, mask, gn, og, out):
+    nc = tc.nc
+    with ExitStack() as ctx:
+        sb = ctx.enter_context(tc.tile_pool(name="sb", bufs=1))
+        ps = ctx.enter_context(tc.psum_pool(name="ps", bufs=1))
+        ctx.enter_context(tc.manual_schedule())
+
+        def tl(name, shape, dtype):
+            return sb.tile(shape, dtype, name=name, align_bytes=64)
+
+        t_sb = tl("t_sb", [P, PACK], F32)
+        k_raw = tl("k_raw", [P, PACK, N], F32)
+        q_raw = [tl("q_raw%d" % c, [P, PACK, HALF], F32) for c in range(2)]
+        m_raw = [tl("m_raw%d" % c, [P, PACK, HALF], F32) for c in range(2)]
+        v_raw = tl("v_raw", [P, H, PACK, E], F32)
+        gn_sb = tl("gn_sb", [P, E], F32)
+        og_sb = tl("og_sb", [P, H, BLOCKS, E], F32)
+
+        q_rows = qT.rearrange("h (p j) n -> (h p) j n", j=PACK)
+        k_rows = kT.rearrange("h (p j) n -> (h p) j n", j=PACK)
+        m_rows = mask.rearrange("(p j) n -> p j n", j=PACK)
+        nc.sync.dma_start(out=k_raw[:], in_=k_rows)
+        nc.sync.dma_start(out=q_raw[0][:], in_=q_rows[:, :, 0:HALF])
+        nc.sync.dma_start(out=q_raw[1][:], in_=q_rows[:, :, HALF:NQ])
+        nc.sync.dma_start(out=t_sb[:], in_=t.rearrange("(p j) o -> p (j o)", j=PACK))
+        nc.sync.dma_start(out=m_raw[0][:], in_=m_rows[:, :, 0:HALF])
+        nc.sync.dma_start(out=v_raw[:], in_=v.rearrange("h (p j) e -> p h j e", j=PACK))
+        nc.sync.dma_start(out=m_raw[1][:], in_=m_rows[:, :, HALF:NQ])
+        nc.sync.dma_start(out=og_sb[:], in_=og.rearrange("h (b p) e -> p h b e", p=P))
+        nc.sync.dma_start(out=gn_sb[:], in_=gn)
+
+        warm_in = tl("warm_in", [P, 1], F32)
+        warm_out = tl("warm_out", [P, 1], F32)
+        nc.vector.memset(warm_in[:], 0.0)
+        nc.scalar.activation(out=warm_out[:], in_=warm_in[:], func=ACT.Sigmoid)
+
+        k_bf = tl("k_bf", [P, N * PACK], BF16)
+        k_codes = tl("k_codes", [P, N], U32)
+        k_scales = tl("k_scales", [P, N], U8)
+        q_bf = [tl("q_bf%d" % b, [P, QB * PACK], BF16) for b in range(BLOCKS)]
+        q_codes = [tl("q_codes%d" % b, [P, QB], U32) for b in range(BLOCKS)]
+        q_scales = [tl("q_scales%d" % b, [P, QB], U8) for b in range(BLOCKS)]
+        v_bf = tl("v_bf", [P, H * E * PACK], BF16)
+        v_codes = tl("v_codes", [P, H * E], U32)
+        v_scales = tl("v_scales", [P, H * E], U8)
+        mt = [tl("mt%d" % c, [P, PACK, HALF], F32) for c in range(2)]
+        pairs = [(b, h) for b in range(BLOCKS) for h in range(H)]
+        p_sb = {x: tl("p_%d%d" % x, [P, QB * PACK], F32) for x in pairs}
+        w_bf = {x: tl("w_bf%d%d" % x, [P, QB * PACK], BF16) for x in pairs}
+        w_codes = {x: tl("w_codes%d%d" % x, [P, QB], U32) for x in pairs}
+        w_scales = {x: tl("w_scales%d%d" % x, [P, QB], U8) for x in pairs}
+        sq = {x: tl("sq%d%d" % x, [P, E], BF16) for x in pairs}
+        ss = [tl("ss%d" % b, [P, H], F32) for b in range(BLOCKS)]
+        rs = [tl("rs%d" % b, [P, H], F32) for b in range(BLOCKS)]
+        sog = tl("sog", [P, H, BLOCKS, E], F32)
+        gate = [tl("gate%d" % b, [P, H, E], F32) for b in range(BLOCKS)]
+        res = [tl("res%d" % b, [P, H, E], F32) for b in range(BLOCKS)]
+        sc_bank = {(h, u): ps.tile([P, PACK * QB], F32, name="sc%d%d" % (h, u)) for h in range(H) for u in range(2)}
+        y_bank = [ps.tile([P, 4 * E], F32, name="y%d" % b) for b in range(BLOCKS)]
+
+        def copy_on(eng, o, i):
+            if eng == "V":
+                nc.vector.tensor_copy(out=o, in_=i)
+            else:
+                nc.scalar.copy(out=o, in_=i)
+
+        def quant(codes, scales, src):
+            nc.vector.quantize_mx(out=codes[:].bitcast(FP8X4), scales=scales[:], in_=src[:])
+
+        def k_il(eng, s0, s1):
+            o = k_bf[:].rearrange("p (a i s j) -> p a s j i", a=2, i=2, j=PACK)
+            i = k_raw[:].rearrange("p j (s a i) -> p a s j i", a=2, i=2)
+            copy_on(eng, o[:, :, s0:s1], i[:, :, s0:s1])
+
+        def q_il(eng, b):
+            o = q_bf[b][:].rearrange("p (c i j) -> p c j i", i=2, j=PACK)
+            cols = slice((b % 2) * QB, (b % 2 + 1) * QB)
+            i = q_raw[b // 2][:, :, cols].rearrange("p j (c i) -> p c j i", i=2)
+            copy_on(eng, o, i)
+
+        def q_quant(b):
+            quant(q_codes[b], q_scales[b], q_bf[b])
+
+        def v_il(eng):
+            o = v_bf[:].rearrange("p (h c i j) -> p h c j i", h=H, i=2, j=PACK)
+            i = v_raw[:].rearrange("p h j (c i) -> p h c j i", i=2)
+            copy_on(eng, o, i)
+
+        def mask_t(c):
+            for j in range(PACK):
+                nc.vector.tensor_scalar(out=mt[c][:, j, :], in0=m_raw[c][:, j, :], scalar1=t_sb[:, j : j + 1],
+                                        scalar2=None, op0=ALU.mult)
+
+        def scores(b):
+            for r in range(PACK):
+                cols = slice(r * QB, (r + 1) * QB)
+                for h in range(H):
+                    rows = slice(ROWS * h, ROWS * (h + 1))
+                    nc.tensor.matmul_mx(
+                        out=sc_bank[h, b % 2][:, cols],
+                        lhsT=k_codes[rows, cols].bitcast(FP8X4),
+                        lhsT_scale=k_scales[rows, cols],
+                        rhs=q_codes[b][rows, :].bitcast(FP8X4),
+                        rhs_scale=q_scales[b][rows, :],
+                        start=True,
+                        stop=True,
+                    )
+
+        def sigm(b, h):
+            nc.scalar.activation(
+                out=p_sb[b, h][:].rearrange("p (c j i) -> p c j i", j=PACK, i=2),
+                in_=sc_bank[h, b % 2][:].rearrange("p (j c i) -> p c j i", j=PACK, i=2),
+                func=ACT.Sigmoid,
+            )
+
+        def weigh(b, h):
+            cols = slice((b % 2) * QB, (b % 2 + 1) * QB)
+            nc.vector.tensor_tensor(
+                out=w_bf[b, h][:].rearrange("p (c i j) -> p c j i", i=2, j=PACK),
+                in0=p_sb[b, h][:].rearrange("p (c j i) -> p c j i", j=PACK, i=2),
+                in1=mt[b // 2][:, :, cols].rearrange("p j (c i) -> p c j i", i=2),
+                op=ALU.mult,
+            )
+
+        def w_quant(b, h):
+            quant(w_codes[b, h], w_scales[b, h], w_bf[b, h])
+
+        def values(b, h):
+            cols = slice(h * E, (h + 1) * E)
+            nc.tensor.matmul_mx(
+                out=y_bank[b][:, cols],
+                lhsT=w_codes[b, h][:].bitcast(FP8X4),
+                lhsT_scale=w_scales[b, h][:],
+                rhs=v_codes[:, cols].bitcast(FP8X4),
+                rhs_scale=v_scales[:, cols],
+                start=True,
+                stop=True,
+            )
+
+        def square(b, h):
+            nc.scalar.activation(out=sq[b, h][:], in_=y_bank[b][:, h * E : (h + 1) * E], func=ACT.Square,
+                                 accum_out=ss[b][:, h : h + 1])
+
+        def root(b):
+            nc.scalar.activation(out=rs[b][:], in_=ss[b][:], func=ACT.Abs_reciprocal_sqrt, scale=1.0 / E,
+                                 bias=256.0 * 1e-5)
+
+        def make_gate(b):
+            nc.vector.tensor_tensor(out=gate[b][:], in0=sog[:, :, b, :],
+                                    in1=gn_sb[:].unsqueeze(1).to_broadcast([P, H, E]), op=ALU.mult)
+
+        def finish(b):
+            for h in range(H):
+                nc.vector.scalar_tensor_tensor(out=res[b][:, h, :], in0=y_bank[b][:, h * E : (h + 1) * E],
+                                               scalar=rs[b][:, h : h + 1], in1=gate[b][:, h, :],
+                                               op0=ALU.mult, op1=ALU.mult)
+            nc.sync.dma_start(out=out[:, b * QB : (b + 1) * QB, :].rearrange("h p e -> p h e"), in_=res[b][:])
+
+        k_il("V", 0, K_SPLIT)
+        k_il("S", K_SPLIT, P)
+        quant(k_codes, k_scales, k_bf)
+        q_il("V", 0)
+        q_il("S", 1)
+        q_quant(0)
+        q_quant(1)
+        scores(0)
+        scores(1)
+        q_il("V", 3)
+        q_il("S", 2)
+        q_quant(3)
+        q_quant(2)
+        mask_t(0)
+        sigm(0, 0)
+        sigm(0, 1)
+        scores(2)
+        sigm(1, 0)
+        sigm(1, 1)
+        scores(3)
+        v_il("S")
+        weigh(0, 0)
+        weigh(0, 1)
+        w_quant(0, 0)
+        weigh(1, 0)
+        w_quant(0, 1)
+        weigh(1, 1)
+        w_quant(1, 0)
+        quant(v_codes, v_scales, v_bf)
+        w_quant(1, 1)
+        mask_t(1)
+        for b in (2, 3):
+            sigm(b, 0)
+            sigm(b, 1)
+        for b in (0, 1):
+            values(b, 0)
+            values(b, 1)
+        for b in (0, 1):
+            square(b, 0)
+            square(b, 1)
+        nc.scalar.activation(out=sog[:], in_=og_sb[:], func=ACT.Sigmoid)
+        root(0)
+        root(1)
+        weigh(2, 0)
+        weigh(2, 1)
+        w_quant(2, 0)
+        weigh(3, 0)
+        w_quant(2, 1)
+        weigh(3, 1)
+        w_quant(3, 0)
+        make_gate(0)
+        w_quant(3, 1)
+        for b in (2, 3):
+            values(b, 0)
+            values(b, 1)
+            square(b, 0)
+            square(b, 1)
+            root(b)
+        make_gate(1)
+        finish(0)
+        make_gate(2)
+        finish(1)
+        make_gate(3)
+        finish(2)
+        finish(3)

@@ -44,9 +44,9 @@ def tile_rows_a_sigmoid_mask_onorm_gate_kernel(tc, qT, kT, t, v, mask, gn, og, o
         k_rows = kT.rearrange("h (p j) n -> (h p) j n", j=PACK)
         m_rows = mask.rearrange("(p j) n -> p j n", j=PACK)
         nc.sync.dma_start(out=k_raw[:], in_=k_rows)
+        nc.scalar.dma_start(out=t_sb[:], in_=t.rearrange("(p j) o -> p (j o)", j=PACK))
         nc.sync.dma_start(out=q_raw[0][:], in_=q_rows[:, :, 0:HALF])
         nc.sync.dma_start(out=q_raw[1][:], in_=q_rows[:, :, HALF:NQ])
-        nc.sync.dma_start(out=t_sb[:], in_=t.rearrange("(p j) o -> p (j o)", j=PACK))
         nc.sync.dma_start(out=m_raw[0][:], in_=m_rows[:, :, 0:HALF])
         nc.sync.dma_start(out=v_raw[:], in_=v.rearrange("h (p j) e -> p h j e", j=PACK))
         nc.sync.dma_start(out=m_raw[1][:], in_=m_rows[:, :, HALF:NQ])
@@ -81,6 +81,9 @@ def tile_rows_a_sigmoid_mask_onorm_gate_kernel(tc, qT, kT, t, v, mask, gn, og, o
         res = [tl("res%d" % b, [P, H, E], F32) for b in range(BLOCKS)]
         sc_bank = {(h, u): ps.tile([P, PACK * QB], F32, name="sc%d%d" % (h, u)) for h in range(H) for u in range(2)}
         y_bank = [ps.tile([P, 4 * E], F32, name="y%d" % b) for b in range(BLOCKS)]
+        place = {(0, 0): (0, 0), (0, 1): (0, 1), (1, 0): (0, 2), (1, 1): (0, 3), (2, 0): (1, 0), (2, 1): (1, 1),
+                 (3, 0): (2, 0), (3, 1): (3, 0)}
+        y_ps = {x: y_bank[place[x][0]][:, place[x][1] * E : (place[x][1] + 1) * E] for x in pairs}
 
         def copy_on(eng, o, i):
             if eng == "V":
@@ -115,10 +118,10 @@ def tile_rows_a_sigmoid_mask_onorm_gate_kernel(tc, qT, kT, t, v, mask, gn, og, o
                 nc.vector.tensor_scalar(out=mt[c][:, j, :], in0=m_raw[c][:, j, :], scalar1=t_sb[:, j : j + 1],
                                         scalar2=None, op0=ALU.mult)
 
-        def scores(b):
+        def scores(b, hs):
             for r in range(PACK):
                 cols = slice(r * QB, (r + 1) * QB)
-                for h in range(H):
+                for h in hs:
                     rows = slice(ROWS * h, ROWS * (h + 1))
                     nc.tensor.matmul_mx(
                         out=sc_bank[h, b % 2][:, cols],
@@ -152,7 +155,7 @@ def tile_rows_a_sigmoid_mask_onorm_gate_kernel(tc, qT, kT, t, v, mask, gn, og, o
         def values(b, h):
             cols = slice(h * E, (h + 1) * E)
             nc.tensor.matmul_mx(
-                out=y_bank[b][:, cols],
+                out=y_ps[b, h],
                 lhsT=w_codes[b, h][:].bitcast(FP8X4),
                 lhsT_scale=w_scales[b, h][:],
                 rhs=v_codes[:, cols].bitcast(FP8X4),
@@ -162,7 +165,7 @@ def tile_rows_a_sigmoid_mask_onorm_gate_kernel(tc, qT, kT, t, v, mask, gn, og, o
             )
 
         def square(b, h):
-            nc.scalar.activation(out=sq[b, h][:], in_=y_bank[b][:, h * E : (h + 1) * E], func=ACT.Square,
+            nc.scalar.activation(out=sq[b, h][:], in_=y_ps[b, h], func=ACT.Square,
                                  accum_out=ss[b][:, h : h + 1])
 
         def root(b):
@@ -175,10 +178,13 @@ def tile_rows_a_sigmoid_mask_onorm_gate_kernel(tc, qT, kT, t, v, mask, gn, og, o
 
         def finish(b):
             for h in range(H):
-                nc.vector.scalar_tensor_tensor(out=res[b][:, h, :], in0=y_bank[b][:, h * E : (h + 1) * E],
+                nc.vector.scalar_tensor_tensor(out=res[b][:, h, :], in0=y_ps[b, h],
                                                scalar=rs[b][:, h : h + 1], in1=gate[b][:, h, :],
                                                op0=ALU.mult, op1=ALU.mult)
-            nc.sync.dma_start(out=out[:, b * QB : (b + 1) * QB, :].rearrange("h p e -> p h e"), in_=res[b][:])
+                if b == BLOCKS - 1:
+                    (nc.sync, nc.scalar)[h].dma_start(out=out[h, b * QB : (b + 1) * QB, :], in_=res[b][:, h, :])
+            if b < BLOCKS - 1:
+                nc.sync.dma_start(out=out[:, b * QB : (b + 1) * QB, :].rearrange("h p e -> p h e"), in_=res[b][:])
 
         k_il("V", 0, K_SPLIT)
         k_il("S", K_SPLIT, P)
@@ -187,20 +193,22 @@ def tile_rows_a_sigmoid_mask_onorm_gate_kernel(tc, qT, kT, t, v, mask, gn, og, o
         q_il("S", 1)
         q_quant(0)
         q_quant(1)
-        scores(0)
-        scores(1)
+        for b in (0, 1):
+            scores(b, [0])
+            scores(b, [1])
+        q_il("V", 2)
         q_il("V", 3)
-        q_il("S", 2)
-        q_quant(3)
         q_quant(2)
+        q_quant(3)
         mask_t(0)
-        sigm(0, 0)
-        sigm(0, 1)
-        scores(2)
-        sigm(1, 0)
-        sigm(1, 1)
-        scores(3)
+        for b in (0, 1):
+            for h in range(H):
+                sigm(b, h)
+                scores(b + 2, [h])
         v_il("S")
+        for b in (2, 3):
+            sigm(b, 0)
+            sigm(b, 1)
         weigh(0, 0)
         weigh(0, 1)
         w_quant(0, 0)
@@ -209,35 +217,37 @@ def tile_rows_a_sigmoid_mask_onorm_gate_kernel(tc, qT, kT, t, v, mask, gn, og, o
         weigh(1, 1)
         w_quant(1, 0)
         quant(v_codes, v_scales, v_bf)
-        w_quant(1, 1)
         mask_t(1)
-        for b in (2, 3):
-            sigm(b, 0)
-            sigm(b, 1)
+        w_quant(1, 1)
         for b in (0, 1):
             values(b, 0)
             values(b, 1)
-        for b in (0, 1):
-            square(b, 0)
-            square(b, 1)
         nc.scalar.activation(out=sog[:], in_=og_sb[:], func=ACT.Sigmoid)
+        square(0, 0)
+        square(0, 1)
         root(0)
-        root(1)
+        square(1, 0)
+        square(1, 1)
         weigh(2, 0)
         weigh(2, 1)
         w_quant(2, 0)
+        values(2, 0)
         weigh(3, 0)
         w_quant(2, 1)
+        values(2, 1)
         weigh(3, 1)
         w_quant(3, 0)
+        values(3, 0)
         make_gate(0)
         w_quant(3, 1)
-        for b in (2, 3):
-            values(b, 0)
-            values(b, 1)
-            square(b, 0)
-            square(b, 1)
-            root(b)
+        values(3, 1)
+        square(2, 0)
+        root(1)
+        square(2, 1)
+        square(3, 0)
+        root(2)
+        square(3, 1)
+        root(3)
         make_gate(1)
         finish(0)
         make_gate(2)

@@ -16,242 +16,230 @@ ALU = mybir.AluOpType
 P = 128
 PACK = 4
 ROWS = D // PACK
-QB = 128
-BLOCKS = NQ // QB
-HALF = NQ // 2
-K_SPLIT = 88
+COLS = 128
+PAIRS = 2
+BETWEEN_COLS = 32
+Y_DIVISOR = 16.0
+EPS = 1e-5
 
 
 def tile_rows_a_sigmoid_mask_onorm_gate_kernel(tc, qT, kT, t, v, mask, gn, og, out):
     nc = tc.nc
+    groups = [(a, h) for a in range(PAIRS) for h in range(H)]
+    units = [(g, u) for g in range(len(groups)) for u in range(2)]
+
     with ExitStack() as ctx:
         sb = ctx.enter_context(tc.tile_pool(name="sb", bufs=1))
         ps = ctx.enter_context(tc.psum_pool(name="ps", bufs=1))
         ctx.enter_context(tc.manual_schedule())
 
-        def tl(name, shape, dtype):
+        def tile(name, shape, dtype):
             return sb.tile(shape, dtype, name=name, align_bytes=64)
 
-        t_sb = tl("t_sb", [P, PACK], F32)
-        k_raw = tl("k_raw", [P, PACK, N], F32)
-        q_raw = [tl("q_raw%d" % c, [P, PACK, HALF], F32) for c in range(2)]
-        m_raw = [tl("m_raw%d" % c, [P, PACK, HALF], F32) for c in range(2)]
-        v_raw = tl("v_raw", [P, H, PACK, E], F32)
-        gn_sb = tl("gn_sb", [P, E], F32)
-        og_sb = tl("og_sb", [P, H, BLOCKS, E], F32)
+        def mx_tiles(name, words):
+            return tile(name + "_codes", [P, words], U32), tile(name + "_scales", [P, words], U8)
 
-        q_rows = qT.rearrange("h (p j) n -> (h p) j n", j=PACK)
-        k_rows = kT.rearrange("h (p j) n -> (h p) j n", j=PACK)
-        m_rows = mask.rearrange("(p j) n -> p j n", j=PACK)
-        nc.sync.dma_start(out=k_raw[:], in_=k_rows)
-        nc.scalar.dma_start(out=t_sb[:], in_=t.rearrange("(p j) o -> p (j o)", j=PACK))
-        nc.sync.dma_start(out=q_raw[0][:], in_=q_rows[:, :, 0:HALF])
-        nc.sync.dma_start(out=q_raw[1][:], in_=q_rows[:, :, HALF:NQ])
-        nc.sync.dma_start(out=m_raw[0][:], in_=m_rows[:, :, 0:HALF])
-        nc.sync.dma_start(out=v_raw[:], in_=v.rearrange("h (p j) e -> p h j e", j=PACK))
-        nc.sync.dma_start(out=m_raw[1][:], in_=m_rows[:, :, HALF:NQ])
-        nc.sync.dma_start(out=og_sb[:], in_=og.rearrange("h (b p) e -> p h b e", p=P))
-        nc.sync.dma_start(out=gn_sb[:], in_=gn)
+        def quantise(mx, src):
+            nc.vector.quantize_mx(out=mx[0][:].bitcast(FP8X4), scales=mx[1][:], in_=src)
 
-        warm_in = tl("warm_in", [P, 1], F32)
-        warm_out = tl("warm_out", [P, 1], F32)
-        nc.vector.memset(warm_in[:], 0.0)
-        nc.scalar.activation(out=warm_out[:], in_=warm_in[:], func=ACT.Sigmoid)
-
-        k_bf = tl("k_bf", [P, N * PACK], BF16)
-        k_codes = tl("k_codes", [P, N], U32)
-        k_scales = tl("k_scales", [P, N], U8)
-        q_bf = [tl("q_bf%d" % b, [P, QB * PACK], BF16) for b in range(BLOCKS)]
-        q_codes = [tl("q_codes%d" % b, [P, QB], U32) for b in range(BLOCKS)]
-        q_scales = [tl("q_scales%d" % b, [P, QB], U8) for b in range(BLOCKS)]
-        v_bf = tl("v_bf", [P, H * E * PACK], BF16)
-        v_codes = tl("v_codes", [P, H * E], U32)
-        v_scales = tl("v_scales", [P, H * E], U8)
-        mt = [tl("mt%d" % c, [P, PACK, HALF], F32) for c in range(2)]
-        pairs = [(b, h) for b in range(BLOCKS) for h in range(H)]
-        p_sb = {x: tl("p_%d%d" % x, [P, QB * PACK], F32) for x in pairs}
-        w_bf = {x: tl("w_bf%d%d" % x, [P, QB * PACK], BF16) for x in pairs}
-        w_codes = {x: tl("w_codes%d%d" % x, [P, QB], U32) for x in pairs}
-        w_scales = {x: tl("w_scales%d%d" % x, [P, QB], U8) for x in pairs}
-        sq = {x: tl("sq%d%d" % x, [P, E], BF16) for x in pairs}
-        ss = [tl("ss%d" % b, [P, H], F32) for b in range(BLOCKS)]
-        rs = [tl("rs%d" % b, [P, H], F32) for b in range(BLOCKS)]
-        sog = tl("sog", [P, H, BLOCKS, E], F32)
-        gate = [tl("gate%d" % b, [P, H, E], F32) for b in range(BLOCKS)]
-        res = [tl("res%d" % b, [P, H, E], F32) for b in range(BLOCKS)]
-        sc_bank = {(h, u): ps.tile([P, PACK * QB], F32, name="sc%d%d" % (h, u)) for h in range(H) for u in range(2)}
-        y_bank = [ps.tile([P, 4 * E], F32, name="y%d" % b) for b in range(BLOCKS)]
-        place = {(0, 0): (0, 0), (0, 1): (0, 1), (1, 0): (0, 2), (1, 1): (0, 3), (2, 0): (1, 0), (2, 1): (1, 1),
-                 (3, 0): (2, 0), (3, 1): (3, 0)}
-        y_ps = {x: y_bank[place[x][0]][:, place[x][1] * E : (place[x][1] + 1) * E] for x in pairs}
-
-        def copy_on(eng, o, i):
-            if eng == "V":
-                nc.vector.tensor_copy(out=o, in_=i)
-            else:
-                nc.scalar.copy(out=o, in_=i)
-
-        def quant(codes, scales, src):
-            nc.vector.quantize_mx(out=codes[:].bitcast(FP8X4), scales=scales[:], in_=src[:])
-
-        def k_il(eng, s0, s1):
-            o = k_bf[:].rearrange("p (a i s j) -> p a s j i", a=2, i=2, j=PACK)
-            i = k_raw[:].rearrange("p j (s a i) -> p a s j i", a=2, i=2)
-            copy_on(eng, o[:, :, s0:s1], i[:, :, s0:s1])
-
-        def q_il(eng, b):
-            o = q_bf[b][:].rearrange("p (c i j) -> p c j i", i=2, j=PACK)
-            cols = slice((b % 2) * QB, (b % 2 + 1) * QB)
-            i = q_raw[b // 2][:, :, cols].rearrange("p j (c i) -> p c j i", i=2)
-            copy_on(eng, o, i)
-
-        def q_quant(b):
-            quant(q_codes[b], q_scales[b], q_bf[b])
-
-        def v_il(eng):
-            o = v_bf[:].rearrange("p (h c i j) -> p h c j i", h=H, i=2, j=PACK)
-            i = v_raw[:].rearrange("p h j (c i) -> p h c j i", i=2)
-            copy_on(eng, o, i)
-
-        def mask_t(c):
-            for j in range(PACK):
-                nc.vector.tensor_scalar(out=mt[c][:, j, :], in0=m_raw[c][:, j, :], scalar1=t_sb[:, j : j + 1],
-                                        scalar2=None, op0=ALU.mult)
-
-        def scores(b, hs):
-            for r in range(PACK):
-                cols = slice(r * QB, (r + 1) * QB)
-                for h in hs:
-                    rows = slice(ROWS * h, ROWS * (h + 1))
-                    nc.tensor.matmul_mx(
-                        out=sc_bank[h, b % 2][:, cols],
-                        lhsT=k_codes[rows, cols].bitcast(FP8X4),
-                        lhsT_scale=k_scales[rows, cols],
-                        rhs=q_codes[b][rows, :].bitcast(FP8X4),
-                        rhs_scale=q_scales[b][rows, :],
-                        start=True,
-                        stop=True,
-                    )
-
-        def sigm(b, h):
-            nc.scalar.activation(
-                out=p_sb[b, h][:].rearrange("p (c j i) -> p c j i", j=PACK, i=2),
-                in_=sc_bank[h, b % 2][:].rearrange("p (j c i) -> p c j i", j=PACK, i=2),
-                func=ACT.Sigmoid,
-            )
-
-        def weigh(b, h):
-            cols = slice((b % 2) * QB, (b % 2 + 1) * QB)
-            nc.vector.tensor_tensor(
-                out=w_bf[b, h][:].rearrange("p (c i j) -> p c j i", i=2, j=PACK),
-                in0=p_sb[b, h][:].rearrange("p (c j i) -> p c j i", j=PACK, i=2),
-                in1=mt[b // 2][:, :, cols].rearrange("p j (c i) -> p c j i", i=2),
-                op=ALU.mult,
-            )
-
-        def w_quant(b, h):
-            quant(w_codes[b, h], w_scales[b, h], w_bf[b, h])
-
-        def values(b, h):
-            cols = slice(h * E, (h + 1) * E)
+        def matmul(dst, lhs, lhs_cols, rhs, rhs_cols, rows):
             nc.tensor.matmul_mx(
-                out=y_ps[b, h],
-                lhsT=w_codes[b, h][:].bitcast(FP8X4),
-                lhsT_scale=w_scales[b, h][:],
-                rhs=v_codes[:, cols].bitcast(FP8X4),
-                rhs_scale=v_scales[:, cols],
+                out=dst,
+                lhsT=lhs[0][rows, lhs_cols].bitcast(FP8X4),
+                lhsT_scale=lhs[1][rows, lhs_cols],
+                rhs=rhs[0][rows, rhs_cols].bitcast(FP8X4),
+                rhs_scale=rhs[1][rows, rhs_cols],
                 start=True,
                 stop=True,
             )
 
-        def square(b, h):
-            nc.scalar.activation(out=sq[b, h][:], in_=y_ps[b, h], func=ACT.Square,
-                                 accum_out=ss[b][:, h : h + 1])
+        def window(n, width):
+            return slice(n * width, (n + 1) * width)
 
-        def root(b):
-            nc.scalar.activation(out=rs[b][:], in_=ss[b][:], func=ACT.Abs_reciprocal_sqrt, scale=1.0 / E,
-                                 bias=256.0 * 1e-5)
+        k_raw = tile("k_raw", [P, PACK, N], F32)
+        t_sb = tile("t_sb", [P, PACK], F32)
+        q_raw = tile("q_raw", [P, PACK, NQ], F32)
+        mask_parts = [(0, 2), (2, 3), (3, 4)]
+        mask_raw = [tile("mask_raw%d" % j0, [P, j1 - j0, NQ], F32) for j0, j1 in mask_parts]
+        v_raw = tile("v_raw", [P, H, PACK, E], F32)
+        og_sb = tile("og_sb", [P, H, PACK, E], F32)
+        gn_sb = tile("gn_sb", [P, E], F32)
+        nc.sync.dma_start(out=k_raw[:], in_=kT.rearrange("h (p j) n -> (h p) j n", j=PACK))
+        nc.scalar.dma_start(out=t_sb[:], in_=t.rearrange("(p j) o -> p (j o)", j=PACK))
+        nc.sync.dma_start(out=q_raw[:], in_=qT.rearrange("h (p j) n -> (h p) j n", j=PACK))
+        mask_rows = mask.rearrange("(p j) n -> p j n", j=PACK)
+        mask_place = []
+        for part, (j0, j1) in zip(mask_raw, mask_parts):
+            nc.sync.dma_start(out=part[:], in_=mask_rows[:, j0:j1, :])
+            mask_place.extend(part[:, j - j0, :] for j in range(j0, j1))
+        nc.sync.dma_start(out=v_raw[:], in_=v.rearrange("h (p j) e -> p h j e", j=PACK))
+        nc.sync.dma_start(out=og_sb[:], in_=og.rearrange("h (m b) e -> m h b e", b=PACK))
+        nc.sync.dma_start(out=gn_sb[:], in_=gn)
 
-        def make_gate(b):
-            nc.vector.tensor_tensor(out=gate[b][:], in0=sog[:, :, b, :],
-                                    in1=gn_sb[:].unsqueeze(1).to_broadcast([P, H, E]), op=ALU.mult)
+        k_bf = [tile("k_bf%d" % a, [P, 2 * COLS * PACK], BF16) for a in range(PAIRS)]
+        k_mx = [mx_tiles("k%d" % a, 2 * COLS) for a in range(PAIRS)]
+        q_bf = [tile("q_bf%d" % a, [P, 2 * COLS * PACK], BF16) for a in range(PAIRS)]
+        q_mx = [mx_tiles("q%d" % b, COLS) for b in range(PACK)]
+        v_bf = tile("v_bf", [P, H * E * PACK], BF16)
+        v_mx = mx_tiles("v", H * E)
+        mask_t = tile("mask_t", [P, PACK, PACK, COLS], F32)
+        probs = {x: tile("probs%d%d" % x, [P, COLS * PACK], F32) for x in units}
+        w_bf = {x: tile("w_bf%d%d" % x, [P, COLS * PACK], BF16) for x in units}
+        w_mx = {x: mx_tiles("w%d%d" % x, COLS) for x in units}
+        squares = {x: tile("squares%d%d" % x, [P, E], BF16) for x in units}
+        square_sum = [tile("square_sum%d" % g, [P, 2], F32) for g in range(len(groups))]
+        inv_rms = [tile("inv_rms%d" % g, [P, 2], F32) for g in range(len(groups))]
+        og_sig = tile("og_sig", [P, H, PACK, E], F32)
+        gate = [tile("gate%d" % g, [P, 2, E], F32) for g in range(len(groups))]
+        res = [tile("res%d" % g, [P, 2, E], F32) for g in range(len(groups))]
 
-        def finish(b):
-            for h in range(H):
-                nc.vector.scalar_tensor_tensor(out=res[b][:, h, :], in0=y_ps[b, h],
-                                               scalar=rs[b][:, h : h + 1], in1=gate[b][:, h, :],
-                                               op0=ALU.mult, op1=ALU.mult)
-                if b == BLOCKS - 1:
-                    (nc.sync, nc.scalar)[h].dma_start(out=out[h, b * QB : (b + 1) * QB, :], in_=res[b][:, h, :])
-            if b < BLOCKS - 1:
-                nc.sync.dma_start(out=out[:, b * QB : (b + 1) * QB, :].rearrange("h p e -> p h e"), in_=res[b][:])
+        score_bank = {
+            (h, u): ps.tile([P, PACK * COLS], F32, name="score%d%d" % (h, u)) for h in range(H) for u in range(2)
+        }
+        y_banks = [ps.tile([P, PACK * E], F32, name="y%d" % n) for n in range(4)]
+        y_ps = {}
+        for bank, members in zip(y_banks, (units[0:2], units[2:6], units[6:7], units[7:8])):
+            for n, x in enumerate(members):
+                y_ps[x] = bank[:, window(n, E)]
 
-        k_il("V", 0, K_SPLIT)
-        k_il("S", K_SPLIT, P)
-        quant(k_codes, k_scales, k_bf)
-        q_il("V", 0)
-        q_il("S", 1)
-        q_quant(0)
-        q_quant(1)
-        for b in (0, 1):
-            scores(b, [0])
-            scores(b, [1])
-        q_il("V", 2)
-        q_il("V", 3)
-        q_quant(2)
-        q_quant(3)
-        mask_t(0)
-        for b in (0, 1):
-            for h in range(H):
-                sigm(b, h)
-                scores(b + 2, [h])
-        v_il("S")
+        def deal(dst, raw, a, s0, s1):
+            src = raw[:].rearrange("p j (s a i) -> p a s j i", a=PAIRS, i=2)
+            words = dst[a][:].rearrange("p (i s j) -> p s j i", i=2, j=PACK)
+            nc.vector.tensor_copy(out=words[:, s0:s1], in_=src[:, a, s0:s1])
+
+        def quantise_queries(b):
+            quantise(q_mx[b], q_bf[b // 2][:, window(b % 2, COLS * PACK)])
+
+        def scale_mask(j):
+            nc.vector.tensor_scalar(
+                out=mask_t[:, j].rearrange("p (a i) m -> p a m i", a=PAIRS),
+                in0=mask_place[j].rearrange("p (m a i) -> p a m i", a=PAIRS, i=2),
+                scalar1=t_sb[:, j : j + 1],
+                scalar2=None,
+                op0=ALU.mult,
+            )
+
+        def scores(g, u):
+            a, h = groups[g]
+            for j in range(PACK):
+                dst = score_bank[h, u][:, window(j, COLS)]
+                matmul(dst, k_mx[j // 2], window(j % 2, COLS), q_mx[2 * a + u], window(0, COLS), window(h, ROWS))
+
+        def sigmoid(g, u):
+            h = groups[g][1]
+            nc.scalar.activation(
+                out=probs[g, u][:].rearrange("p (c j i) -> p c j i", j=PACK, i=2),
+                in_=score_bank[h, u][:].rearrange("p (j c i) -> p c j i", j=PACK, i=2),
+                func=ACT.Sigmoid,
+            )
+
+        def weigh(g, u):
+            a = groups[g][0]
+            nc.vector.tensor_tensor(
+                out=w_bf[g, u][:].rearrange("p (c i j) -> p c j i", i=2, j=PACK),
+                in0=probs[g, u][:].rearrange("p (c j i) -> p c j i", j=PACK, i=2),
+                in1=mask_t[:, :, 2 * a + u, :].rearrange("p j (c i) -> p c j i", i=2),
+                op=ALU.mult,
+            )
+
+        def quantise_weights(g, u):
+            quantise(w_mx[g, u], w_bf[g, u][:])
+
+        def values(g, u):
+            h = groups[g][1]
+            matmul(y_ps[g, u], w_mx[g, u], window(0, COLS), v_mx, window(h, E), window(0, P))
+
+        def square(g, u):
+            nc.scalar.activation(
+                out=squares[g, u][:], in_=y_ps[g, u], func=ACT.Square, accum_out=square_sum[g][:, u : u + 1]
+            )
+
+        def root(g):
+            nc.scalar.activation(
+                out=inv_rms[g][:],
+                in_=square_sum[g][:],
+                func=ACT.Abs_reciprocal_sqrt,
+                scale=1.0 / E,
+                bias=Y_DIVISOR * Y_DIVISOR * EPS,
+            )
+
+        def make_gate(g):
+            a, h = groups[g]
+            nc.vector.tensor_tensor(
+                out=gate[g][:],
+                in0=og_sig[:, h, window(a, 2), :],
+                in1=gn_sb[:].unsqueeze(1).to_broadcast([P, 2, E]),
+                op=ALU.mult,
+            )
+
+        def finish(g):
+            a, h = groups[g]
+            for u in range(2):
+                nc.vector.scalar_tensor_tensor(
+                    out=res[g][:, u, :],
+                    in0=y_ps[g, u],
+                    scalar=inv_rms[g][:, u : u + 1],
+                    in1=gate[g][:, u, :],
+                    op0=ALU.mult,
+                    op1=ALU.mult,
+                )
+            rows = out[h].rearrange("(m b) e -> m b e", b=PACK)
+            nc.sync.dma_start(out=rows[:, window(a, 2), :], in_=res[g][:])
+
+        for a in range(PAIRS):
+            deal(k_bf, k_raw, a, 0, COLS)
+        for a in range(PAIRS):
+            quantise(k_mx[a], k_bf[a][:])
+        deal(q_bf, q_raw, 0, 0, COLS)
+        deal(q_bf, q_raw, 1, 0, BETWEEN_COLS)
+        quantise_queries(0)
+        quantise_queries(1)
+        for x in units[:4]:
+            scores(*x)
+        deal(q_bf, q_raw, 1, BETWEEN_COLS, COLS)
+
         for b in (2, 3):
-            sigm(b, 0)
-            sigm(b, 1)
-        weigh(0, 0)
-        weigh(0, 1)
-        w_quant(0, 0)
-        weigh(1, 0)
-        w_quant(0, 1)
-        weigh(1, 1)
-        w_quant(1, 0)
-        quant(v_codes, v_scales, v_bf)
-        mask_t(1)
-        w_quant(1, 1)
-        for b in (0, 1):
-            values(b, 0)
-            values(b, 1)
-        nc.scalar.activation(out=sog[:], in_=og_sb[:], func=ACT.Sigmoid)
+            scale_mask(2 * b - 4)
+            scale_mask(2 * b - 3)
+            quantise_queries(b)
+
+        for g, u in units:
+            sigmoid(g, u)
+            if g < H:
+                scores(g + H, u)
+        nc.scalar.activation(out=og_sig[:], in_=og_sb[:], func=ACT.Sigmoid)
+
+        weigh(*units[0])
+        weigh(*units[1])
+        quantise_weights(*units[0])
+        nc.vector.tensor_copy(
+            out=v_bf[:].rearrange("p (h c i j) -> p h c j i", h=H, i=2, j=PACK),
+            in_=v_raw[:].rearrange("p h j (c i) -> p h c j i", i=2),
+        )
+        weigh(*units[2])
+        quantise(v_mx, v_bf[:])
+        values(*units[0])
+        for made, last in zip(units[3:], units[1:]):
+            quantise_weights(*last)
+            values(*last)
+            weigh(*made)
+        quantise_weights(*units[-2])
+        values(*units[-2])
+        make_gate(0)
+        quantise_weights(*units[-1])
+        values(*units[-1])
+
         square(0, 0)
         square(0, 1)
         root(0)
         square(1, 0)
-        square(1, 1)
-        weigh(2, 0)
-        weigh(2, 1)
-        w_quant(2, 0)
-        values(2, 0)
-        weigh(3, 0)
-        w_quant(2, 1)
-        values(2, 1)
-        weigh(3, 1)
-        w_quant(3, 0)
-        values(3, 0)
-        make_gate(0)
-        w_quant(3, 1)
-        values(3, 1)
-        square(2, 0)
-        root(1)
-        square(2, 1)
-        square(3, 0)
-        root(2)
-        square(3, 1)
-        root(3)
-        make_gate(1)
-        finish(0)
-        make_gate(2)
-        finish(1)
-        make_gate(3)
-        finish(2)
-        finish(3)
+        for g in range(1, len(groups)):
+            square(g, 1)
+            if g + 1 < len(groups):
+                square(g + 1, 0)
+            root(g)
+
+        for g in range(len(groups)):
+            if g + 1 < len(groups):
+                make_gate(g + 1)
+            finish(g)

from contextlib import ExitStack

import concourse.mybir as mybir

H, D, NQ, N, E = 2, 256, 512, 512, 128
FLOPS = 2 * H * N * NQ * D + 2 * H * NQ * N * E

F32 = mybir.dt.float32
BF16 = mybir.dt.bfloat16
U32 = mybir.dt.uint32
U8 = mybir.dt.uint8
FP8X4 = mybir.dt.float8_e4m3fn_x4
ACT = mybir.ActivationFunctionType
ALU = mybir.AluOpType

P = 128
PACK = 4
ROWS = D // PACK
COLS = 128
PAIRS = 2
BETWEEN_COLS = 32
Y_DIVISOR = 16.0
EPS = 1e-5


def tile_rows_a_sigmoid_mask_onorm_gate_kernel(tc, qT, kT, t, v, mask, gn, og, out):
    nc = tc.nc
    groups = [(a, h) for a in range(PAIRS) for h in range(H)]
    units = [(g, u) for g in range(len(groups)) for u in range(2)]

    with ExitStack() as ctx:
        sb = ctx.enter_context(tc.tile_pool(name="sb", bufs=1))
        ps = ctx.enter_context(tc.psum_pool(name="ps", bufs=1))
        ctx.enter_context(tc.manual_schedule())

        def tile(name, shape, dtype):
            return sb.tile(shape, dtype, name=name, align_bytes=64)

        def mx_tiles(name, words):
            return tile(name + "_codes", [P, words], U32), tile(name + "_scales", [P, words], U8)

        def quantise(mx, src):
            nc.vector.quantize_mx(out=mx[0][:].bitcast(FP8X4), scales=mx[1][:], in_=src)

        def matmul(dst, lhs, lhs_cols, rhs, rhs_cols, rows):
            nc.tensor.matmul_mx(
                out=dst,
                lhsT=lhs[0][rows, lhs_cols].bitcast(FP8X4),
                lhsT_scale=lhs[1][rows, lhs_cols],
                rhs=rhs[0][rows, rhs_cols].bitcast(FP8X4),
                rhs_scale=rhs[1][rows, rhs_cols],
                start=True,
                stop=True,
            )

        def window(n, width):
            return slice(n * width, (n + 1) * width)

        k_raw = tile("k_raw", [P, PACK, N], F32)
        t_sb = tile("t_sb", [P, PACK], F32)
        q_raw = tile("q_raw", [P, PACK, NQ], F32)
        mask_parts = [(0, 2), (2, 3), (3, 4)]
        mask_raw = [tile("mask_raw%d" % j0, [P, j1 - j0, NQ], F32) for j0, j1 in mask_parts]
        v_raw = tile("v_raw", [P, H, PACK, E], F32)
        og_sb = tile("og_sb", [P, H, PACK, E], F32)
        gn_sb = tile("gn_sb", [P, E], F32)
        nc.sync.dma_start(out=k_raw[:], in_=kT.rearrange("h (p j) n -> (h p) j n", j=PACK))
        nc.scalar.dma_start(out=t_sb[:], in_=t.rearrange("(p j) o -> p (j o)", j=PACK))
        nc.sync.dma_start(out=q_raw[:], in_=qT.rearrange("h (p j) n -> (h p) j n", j=PACK))
        mask_rows = mask.rearrange("(p j) n -> p j n", j=PACK)
        mask_place = []
        for part, (j0, j1) in zip(mask_raw, mask_parts):
            nc.sync.dma_start(out=part[:], in_=mask_rows[:, j0:j1, :])
            mask_place.extend(part[:, j - j0, :] for j in range(j0, j1))
        nc.sync.dma_start(out=v_raw[:], in_=v.rearrange("h (p j) e -> p h j e", j=PACK))
        nc.sync.dma_start(out=og_sb[:], in_=og.rearrange("h (m b) e -> m h b e", b=PACK))
        nc.sync.dma_start(out=gn_sb[:], in_=gn)

        k_bf = [tile("k_bf%d" % a, [P, 2 * COLS * PACK], BF16) for a in range(PAIRS)]
        k_mx = [mx_tiles("k%d" % a, 2 * COLS) for a in range(PAIRS)]
        q_bf = [tile("q_bf%d" % a, [P, 2 * COLS * PACK], BF16) for a in range(PAIRS)]
        q_mx = [mx_tiles("q%d" % b, COLS) for b in range(PACK)]
        v_bf = tile("v_bf", [P, H * E * PACK], BF16)
        v_mx = mx_tiles("v", H * E)
        mask_t = tile("mask_t", [P, PACK, PACK, COLS], F32)
        probs = {x: tile("probs%d%d" % x, [P, COLS * PACK], F32) for x in units}
        w_bf = {x: tile("w_bf%d%d" % x, [P, COLS * PACK], BF16) for x in units}
        w_mx = {x: mx_tiles("w%d%d" % x, COLS) for x in units}
        squares = {x: tile("squares%d%d" % x, [P, E], BF16) for x in units}
        square_sum = [tile("square_sum%d" % g, [P, 2], F32) for g in range(len(groups))]
        inv_rms = [tile("inv_rms%d" % g, [P, 2], F32) for g in range(len(groups))]
        og_sig = tile("og_sig", [P, H, PACK, E], F32)
        gate = [tile("gate%d" % g, [P, 2, E], F32) for g in range(len(groups))]
        res = [tile("res%d" % g, [P, 2, E], F32) for g in range(len(groups))]

        score_bank = {
            (h, u): ps.tile([P, PACK * COLS], F32, name="score%d%d" % (h, u)) for h in range(H) for u in range(2)
        }
        y_banks = [ps.tile([P, PACK * E], F32, name="y%d" % n) for n in range(4)]
        y_ps = {}
        for bank, members in zip(y_banks, (units[0:2], units[2:6], units[6:7], units[7:8])):
            for n, x in enumerate(members):
                y_ps[x] = bank[:, window(n, E)]

        def deal(dst, raw, a, s0, s1):
            src = raw[:].rearrange("p j (s a i) -> p a s j i", a=PAIRS, i=2)
            words = dst[a][:].rearrange("p (i s j) -> p s j i", i=2, j=PACK)
            nc.vector.tensor_copy(out=words[:, s0:s1], in_=src[:, a, s0:s1])

        def quantise_queries(b):
            quantise(q_mx[b], q_bf[b // 2][:, window(b % 2, COLS * PACK)])

        def scale_mask(j):
            nc.vector.tensor_scalar(
                out=mask_t[:, j].rearrange("p (a i) m -> p a m i", a=PAIRS),
                in0=mask_place[j].rearrange("p (m a i) -> p a m i", a=PAIRS, i=2),
                scalar1=t_sb[:, j : j + 1],
                scalar2=None,
                op0=ALU.mult,
            )

        def scores(g, u):
            a, h = groups[g]
            for j in range(PACK):
                dst = score_bank[h, u][:, window(j, COLS)]
                matmul(dst, k_mx[j // 2], window(j % 2, COLS), q_mx[2 * a + u], window(0, COLS), window(h, ROWS))

        def sigmoid(g, u):
            h = groups[g][1]
            nc.scalar.activation(
                out=probs[g, u][:].rearrange("p (c j i) -> p c j i", j=PACK, i=2),
                in_=score_bank[h, u][:].rearrange("p (j c i) -> p c j i", j=PACK, i=2),
                func=ACT.Sigmoid,
            )

        def weigh(g, u):
            a = groups[g][0]
            nc.vector.tensor_tensor(
                out=w_bf[g, u][:].rearrange("p (c i j) -> p c j i", i=2, j=PACK),
                in0=probs[g, u][:].rearrange("p (c j i) -> p c j i", j=PACK, i=2),
                in1=mask_t[:, :, 2 * a + u, :].rearrange("p j (c i) -> p c j i", i=2),
                op=ALU.mult,
            )

        def quantise_weights(g, u):
            quantise(w_mx[g, u], w_bf[g, u][:])

        def values(g, u):
            h = groups[g][1]
            matmul(y_ps[g, u], w_mx[g, u], window(0, COLS), v_mx, window(h, E), window(0, P))

        def square(g, u):
            nc.scalar.activation(
                out=squares[g, u][:], in_=y_ps[g, u], func=ACT.Square, accum_out=square_sum[g][:, u : u + 1]
            )

        def root(g):
            nc.scalar.activation(
                out=inv_rms[g][:],
                in_=square_sum[g][:],
                func=ACT.Abs_reciprocal_sqrt,
                scale=1.0 / E,
                bias=Y_DIVISOR * Y_DIVISOR * EPS,
            )

        def make_gate(g):
            a, h = groups[g]
            nc.vector.tensor_tensor(
                out=gate[g][:],
                in0=og_sig[:, h, window(a, 2), :],
                in1=gn_sb[:].unsqueeze(1).to_broadcast([P, 2, E]),
                op=ALU.mult,
            )

        def finish(g):
            a, h = groups[g]
            for u in range(2):
                nc.vector.scalar_tensor_tensor(
                    out=res[g][:, u, :],
                    in0=y_ps[g, u],
                    scalar=inv_rms[g][:, u : u + 1],
                    in1=gate[g][:, u, :],
                    op0=ALU.mult,
                    op1=ALU.mult,
                )
            rows = out[h].rearrange("(m b) e -> m b e", b=PACK)
            nc.sync.dma_start(out=rows[:, window(a, 2), :], in_=res[g][:])

        for a in range(PAIRS):
            deal(k_bf, k_raw, a, 0, COLS)
        for a in range(PAIRS):
            quantise(k_mx[a], k_bf[a][:])
        deal(q_bf, q_raw, 0, 0, COLS)
        deal(q_bf, q_raw, 1, 0, BETWEEN_COLS)
        quantise_queries(0)
        quantise_queries(1)
        for x in units[:4]:
            scores(*x)
        deal(q_bf, q_raw, 1, BETWEEN_COLS, COLS)

        for b in (2, 3):
            scale_mask(2 * b - 4)
            scale_mask(2 * b - 3)
            quantise_queries(b)

        for g, u in units:
            sigmoid(g, u)
            if g < H:
                scores(g + H, u)
        nc.scalar.activation(out=og_sig[:], in_=og_sb[:], func=ACT.Sigmoid)

        weigh(*units[0])
        weigh(*units[1])
        quantise_weights(*units[0])
        nc.vector.tensor_copy(
            out=v_bf[:].rearrange("p (h c i j) -> p h c j i", h=H, i=2, j=PACK),
            in_=v_raw[:].rearrange("p h j (c i) -> p h c j i", i=2),
        )
        weigh(*units[2])
        quantise(v_mx, v_bf[:])
        values(*units[0])
        for made, last in zip(units[3:], units[1:]):
            quantise_weights(*last)
            values(*last)
            weigh(*made)
        quantise_weights(*units[-2])
        values(*units[-2])
        make_gate(0)
        quantise_weights(*units[-1])
        values(*units[-1])

        square(0, 0)
        square(0, 1)
        root(0)
        square(1, 0)
        for g in range(1, len(groups)):
            square(g, 1)
            if g + 1 < len(groups):
                square(g + 1, 0)
            root(g)

        for g in range(len(groups)):
            if g + 1 < len(groups):
                make_gate(g + 1)
            finish(g)
